import numpy as np, ml_dtypes
CORES = [211,219,227,235,243,251,83,91,99,107,115,123]
N = 12
import mx_ref
NC, G = 128, 2
C = np.float32(0.000771)
A = np.float32(0.021)
BF = ml_dtypes.bfloat16
def cut(t, i, w=512):
    return t[:, w * i:w * i + w]
def tile(rs):
    return np.stack(rs, axis=2).reshape(128, -1).astype(BF)
def layer(w, X):
    out = []
    for i in range(G):
        for t in range(len(X)):
            p = mx_ref.matmul(mx_ref.quantize(cut(w, len(X) * i + t)), X[t])
            z = p if t == 0 else z + p
        out.append(z)
    return out
def silu(z):
    z = z.astype(np.float64); e = np.exp(-np.abs(z))
    return (z * np.where(z >= 0, 1, e) / (1 + e)).astype(np.float32)
def gate(U, V):
    return [(silu(s * u * A) * v) * C for u, v in zip(U, V) for s in (1, -1)]
def setup_inputs(rng):
    def f(*shape):
        return mx_ref.flush((rng.standard_normal(shape, dtype=np.float32) * np.exp2(rng.integers(-2, 3, shape[:-1] + (1,)))).astype(BF))
    return {"x": f(N, 128, 4 * NC), "u": f(N, 128, G * 512), "v": f(N, 128, G * 512), "w2": f(N, 128, 512)}
def setup_inputs_blocks(rng):
    d = setup_inputs(rng)
    for k in ("v", "w2"): d[k] = mx_ref.spread(d[k], rng, 4)
    for k in ("x", "u"): d[k] = mx_ref.spread(d[k], rng, 1)
    return d
def setup_inputs_wide(rng):
    d = setup_inputs(rng)
    for k in ("v", "w2"): d[k] = mx_ref.flush((d[k].astype(np.float32) * np.exp2(rng.integers(-5, 6, (N, 1, 1))).astype(np.float32)).astype(BF))
    return d
def setup_inputs_zeros(rng):
    d = setup_inputs(rng); v = d["x"].reshape(N, 128, -1, 4).copy()
    v[np.broadcast_to((rng.random((N, 1, v.shape[2], 1)) < 0.33), v.shape)] = 0
    d["x"] = v.reshape(d["x"].shape)
    return d
def reference(x, u, v, w2, own=None):
    h = np.zeros((N, 128, 4 * NC), BF)
    for j in range(N):
        X = [mx_ref.quantize(x[j])]
        h[j] = tile(gate(layer(u[j], X), layer(v[j], X)))
    use = h if own is None else own["h"]
    H = [mx_ref.quantize(use[j]) for j in range(N)]
    y = np.zeros((N, 128, N * NC), np.float32)
    for r in range(N):
        qw = mx_ref.quantize(w2[r])
        for j in range(N):
            y[r][:, NC * j:NC * j + NC] = mx_ref.matmul(qw, H[j])
    return {"h": h, "y": y}

from concourse.bass import DstId, RemoteDMATransfer
from concourse.mybir import dt, AluOpType, ActivationFunctionType

N = 12
NC = 128
NSIM = 256
A = 0.021
C = 0.000771
NPAIR = N // 2

SCRATCH = {
    "xb": ("sbuf", [128, 512], "bfloat16"),
    "ub": ("sbuf", [128, 1024], "bfloat16"),
    "vb": ("sbuf", [128, 1024], "bfloat16"),
    "wb": ("sbuf", [128, 512], "bfloat16"),
    "xq": ("sbuf", [128, 128], "float8_e4m3fn_x4"),
    "xs": ("sbuf", [128, 128], "uint8"),
    "uq": ("sbuf", [128, 256], "float8_e4m3fn_x4"),
    "us": ("sbuf", [128, 256], "uint8"),
    "vq": ("sbuf", [128, 256], "float8_e4m3fn_x4"),
    "vs": ("sbuf", [128, 256], "uint8"),
    "wq": ("sbuf", [128, 128], "float8_e4m3fn_x4"),
    "ws": ("sbuf", [128, 128], "uint8"),
    "ps": ("psum", [128, 512 * 8], "float32"),
    "sb": ("sbuf", [128, 512], "float32"),
    "pb": ("sbuf", [128, 512], "float32"),
    "hb": ("sbuf", [128, 512], "bfloat16"),
    "HQ": ("sbuf", [128, N * NC], "float8_e4m3fn_x4"),
    "HS": ("sbuf", [128, N * NC], "uint8"),
    "yb": ("sbuf", [128, N * NC], "float32"),
}
SEMAPHORES = (["lx", "lu0", "lu1", "lv0", "lv1", "lw", "qx", "qu0", "qu1", "qv0", "qv1", "qw", "qh",
               "mu0", "mu1", "mv0", "mv1", "hp", "hc", "loc", "sts", "sta"]
              + ["a%d" % b for b in range(4)] + ["p%d" % b for b in range(4)] + ["c%d" % b for b in range(4)]
              + ["r%d" % k for k in range(NPAIR)] + ["my%d" % k for k in range(NPAIR)] + ["e%d" % k for k in range(NPAIR)])

_CACHE = {}


def _bits(mask):
    return bin(mask).count("1")


def _plan(cores, topo):
    if "plan" in _CACHE:
        return _CACHE["plan"]
    n = len(cores)
    pairs, pair_of = [], {}
    for i in range(n):
        if i in pair_of:
            continue
        j = [k for k in range(n) if topo.mates(cores[i], cores[k])][0]
        for t in (i, j):
            pair_of[t] = len(pairs)
        pairs.append((min(i, j), max(i, j)))
    npair = len(pairs)
    jobs, fan, helper = {}, {}, {}
    for s in range(n):
        c = cores[s]
        k = pair_of[s]
        mate = [t for t in pairs[k] if t != s][0]
        same, cross = {}, {}
        for d in range(1, npair):
            for t in pairs[(k + d) % npair]:
                if topo.same_plane(c, cores[t]):
                    same[d] = t
                else:
                    cross[d] = t
        chipc = [w for w in range(NSIM) if w != c and topo.host(w) == topo.host(c) and topo.chip(w) == topo.chip(c)]
        own = [w for w in chipc if topo.die(w) == topo.die(c)]
        oth = [w for w in chipc if topo.die(w) != topo.die(c)]

        def common(w, dests):
            m = topo.mask(w, cores[dests[0]])
            for t in dests:
                m &= topo.mask(w, cores[t])
            return m

        direct = [mate, same[1], cross[1]]
        dmask = common(c, direct)
        taken, hs = [], []
        for pool, dests in ((own, [cross[2], cross[4]]), (oth, [cross[3], cross[5]]),
                            (own, [same[2], same[4]]), (oth, [same[3], same[5]])):
            w = [w for w in pool if w not in taken and all(topo.may_write(w, cores[t]) for t in dests)][0]
            taken.append(w)
            hs.append((w, common(w, dests), dests))
            helper[w] = (s, common(w, dests), dests)
        fmask = topo.mask(c, taken[0])
        for w in taken:
            fmask &= topo.mask(c, w)
        fan[s] = fmask & ~dmask
        jobs[s] = ((dmask, direct), hs)
    plan = {"pairs": pairs, "pair_of": pair_of, "jobs": jobs, "fan": fan, "helper": helper}
    _CACHE["plan"] = plan
    return plan


def _send(g, T, topo, core, cores_to, slot, mask, sem, planes):
    lo, hi = slot * NC, slot * NC + NC
    ap = T.HS[:, lo:hi] if planes else T.HQ[:, lo:hi].bitcast(dt.uint8)
    ids = []
    for d in cores_to:
        rid, pid = topo.addr(d, core)
        ids.append(DstId(rid=rid, pnc=pid))
    g.remote_dma_fused([RemoteDMATransfer(dst_ids=ids, dma_engine_mask=mask, remote_sem=sem, srcs=[ap],
                                          dsts=[ap for d in cores_to])], local_sem=T.sem.loc)


def _helper(g, core, T, topo, plan):
    s, mask, dests = plan["helper"][core]
    arr = T.sem["r%d" % plan["pair_of"][s]]
    to = [T.cores[t] for t in dests]
    n = _bits(plan["fan"][s])
    g.wait_ge(T.sem.hp, n)
    _send(g, T, topo, core, to, s, mask, arr, True)
    g.wait_ge(T.sem.hc, n)
    _send(g, T, topo, core, to, s, mask, arr, False)
    g.wait_ge(T.sem.loc, 2 * _bits(mask))


def rank_program(g, core, T, topo):
    plan = _plan(T.cores, topo)
    if core in plan["helper"]:
        _helper(g, core, T, topo, plan)
        return
    rank = T.rank_of(core)
    if rank is None:
        return
    S = T.sem
    Silu, Copy = ActivationFunctionType.Silu, ActivationFunctionType.Copy
    pairs, pair_of = plan["pairs"], plan["pair_of"]
    k = pair_of[rank]
    npair = len(pairs)

    g.sync.dma_start(T.xb[:], T.x[:]).then_inc(S.lx, 16)
    g.scalar.dma_start(T.ub[:, 0:512], T.u[:, 0:512]).then_inc(S.lu0, 16)
    g.sync.dma_start(T.ub[:, 512:1024], T.u[:, 512:1024]).then_inc(S.lu1, 16)
    g.scalar.dma_start(T.vb[:, 0:512], T.v[:, 0:512]).then_inc(S.lv0, 16)
    g.sync.dma_start(T.vb[:, 512:1024], T.v[:, 512:1024]).then_inc(S.lv1, 16)
    g.sync.dma_start(T.wb[:], T.w2[:]).then_inc(S.lw, 16)

    g.vector.wait_ge(S.lx, 16)
    g.vector.quantize_mx(T.xq[:], T.xs[:], T.xb[:]).then_inc(S.qx, 1)
    g.tensor.wait_ge(S.qx, 1)
    for bank, (ld, qs, ms, q, sc, src, i) in enumerate((
            (S.lu0, S.qu0, S.mu0, T.uq, T.us, T.ub, 0), (S.lu1, S.qu1, S.mu1, T.uq, T.us, T.ub, 1),
            (S.lv0, S.qv0, S.mv0, T.vq, T.vs, T.vb, 0), (S.lv1, S.qv1, S.mv1, T.vq, T.vs, T.vb, 1))):
        g.vector.wait_ge(ld, 16)
        g.vector.quantize_mx(q[:, 128 * i:128 * i + 128], sc[:, 128 * i:128 * i + 128],
                             src[:, 512 * i:512 * i + 512]).then_inc(qs, 1)
        g.tensor.wait_ge(qs, 1)
        g.tensor.matmul_mx(T.ps[:, 512 * bank:512 * bank + 128], q[:, 128 * i:128 * i + 128],
                           sc[:, 128 * i:128 * i + 128], T.xq[:], T.xs[:], True, True).then_inc(ms, 1)

    for b in range(4):
        i = b // 2
        if b % 2 == 0:
            g.scalar.wait_ge((S.mu0, S.mu1)[i], 1)
            g.vector.wait_ge((S.mv0, S.mv1)[i], 1)
        g.scalar.activation(T.sb[:, 128 * b:128 * b + 128], T.ps[:, 512 * i:512 * i + 128], Silu,
                            scale=(A if b % 2 == 0 else -A)).then_inc(S["a%d" % b], 1)
        g.vector.wait_ge(S["a%d" % b], 1)
        g.vector.tensor_tensor(T.pb[:, 128 * b:128 * b + 128], T.sb[:, 128 * b:128 * b + 128],
                               T.ps[:, 512 * (2 + i):512 * (2 + i) + 128], AluOpType.mult).then_inc(S["p%d" % b], 1)
    for b in range(3):
        g.scalar.wait_ge(S["p%d" % b], 1)
        g.scalar.activation(T.hb[:, b:512:4], T.pb[:, 128 * b:128 * b + 128], Copy, scale=C).then_inc(S["c%d" % b], 1)
    g.vector.wait_ge(S.p3, 1)
    g.vector.tensor_scalar(T.hb[:, 3:512:4], T.pb[:, 384:512], C, None, AluOpType.mult).then_inc(S.c3, 1)

    lo = rank * NC
    for b in range(4):
        g.vector.wait_ge(S["c%d" % b], 1)
        g.sync.wait_ge(S["c%d" % b], 1)
    g.vector.quantize_mx(T.HQ[:, lo:lo + NC], T.HS[:, lo:lo + NC], T.hb[:]).then_inc(S.qh, 1)
    g.sync.dma_start(T.h[:], T.hb[:]).then_inc(S.sts, 16)
    nsync = 1
    g.vector.wait_ge(S.lw, 16)
    g.vector.quantize_mx(T.wq[:], T.ws[:], T.wb[:]).then_inc(S.qw, 1)

    (dmask, direct), hs = plan["jobs"][rank]
    fmask = plan["fan"][rank]
    arr = S["r%d" % k]
    hcores = [w for w, m, d in hs]
    dcores = [T.cores[t] for t in direct]
    g.wait_ge(S.qh, 1)
    _send(g, T, topo, core, hcores, rank, fmask, S.hp, True)
    _send(g, T, topo, core, hcores, rank, fmask, S.hc, False)
    _send(g, T, topo, core, dcores, rank, dmask, arr, True)
    _send(g, T, topo, core, dcores, rank, dmask, arr, False)

    def carrier_bits(s):
        (dm, dd), hh = plan["jobs"][s]
        if rank in dd:
            return _bits(dm)
        return [_bits(m) for w, m, d in hh if rank in d][0]

    g.tensor.wait_ge(S.qh, 1)
    g.tensor.wait_ge(S.qw, 1)
    banks = [4, 5, 6, 7, 0, 1]
    nact = 0
    for i in range(npair):
        kk = (k - i) % npair
        a, b = pairs[kk]
        c0, c1 = a * NC, (b + 1) * NC
        w = c1 - c0
        bank = banks[i]
        if bank < 2:
            for t in range(4):
                g.tensor.wait_ge(S["a%d" % t], 1)
        g.tensor.wait_ge(S["r%d" % kk], sum(2 * carrier_bits(s) for s in (a, b) if s != rank))
        g.tensor.matmul_mx(T.ps[:, 512 * bank:512 * bank + w], T.wq[:], T.ws[:], T.HQ[:, c0:c1], T.HS[:, c0:c1],
                           True, True).then_inc(S["my%d" % i], 1)
        if i % 2 == 0:
            g.vector.wait_ge(S["my%d" % i], 1)
            g.vector.tensor_copy(T.yb[:, c0:c1], T.ps[:, 512 * bank:512 * bank + w]).then_inc(S["e%d" % i], 1)
            g.sync.wait_ge(S["e%d" % i], 1)
            g.sync.dma_start(T.y[:, c0:c1], T.yb[:, c0:c1]).then_inc(S.sts, 16)
            nsync += 1
        else:
            g.scalar.wait_ge(S["my%d" % i], 1)
            g.scalar.activation(T.yb[:, c0:c1], T.ps[:, 512 * bank:512 * bank + w], Copy).then_inc(S["e%d" % i], 1)
            g.scalar.wait_ge(S["e%d" % i], 1)
            g.scalar.dma_start(T.y[:, c0:c1], T.yb[:, c0:c1]).then_inc(S.sta, 16)
            nact += 1

    g.wait_ge(S.loc, 2 * _bits(fmask) + 2 * _bits(dmask))
    g.sync.wait_ge(S.sts, 16 * nsync)
    g.scalar.wait_ge(S.sta, 16 * nact)
